import numpy as np, ml_dtypes
CORES = [2,6,10,14,18,22,26,30]
N = 8
BF = ml_dtypes.bfloat16
def gentries(a):
    return np.ascontiguousarray(a.reshape(8, 16, -1).transpose(0, 2, 1)).reshape(8, -1)
def gtable(e):
    e = np.asarray(e); return np.ascontiguousarray(e.reshape(8, -1, 16).transpose(0, 2, 1)).reshape(128, -1).astype(np.int32)
W, B, E, SH, L, H = 4096, 128, 32, 5, 4, 3
R = L * B
def parts(rng):
    Y = rng.integers(0, 256, (N, 8, 16, W)); X = rng.integers(0, 256, (N, 8, 16, R)); m = rng.integers(0, W, (N, 8, R))
    lev = np.arange(B, R) // B; h = []
    for k in range(2):
        at = np.where(rng.random((N, 8, R - B)) < 0.5, 0, (lev * rng.random((N, 8, R - B))).astype(np.int64))
        h.append(rng.integers(0, H + 1, (N, 8, R - B)) * R + at * B + rng.integers(0, B, (N, 8, R - B)))
    a, b = rng.integers(0, W, (N, 8, B)), rng.integers(0, W, (N, 8, B)); far = rng.random((N, 8, B)) < 0.7
    lo = np.where(far, rng.integers(0, W // 4, (N, 8, B)), np.minimum(a, b)); hi = np.where(far, rng.integers(3 * W // 4, W, (N, 8, B)), np.maximum(a, b))
    return Y, X, h[0], h[1], m, lo, hi
def pack(Y, X, a, b, m, lo, hi):
    return {"ytab": np.ascontiguousarray(Y.reshape(N, 128, W)).astype(np.float32).astype(BF), "xrow": np.ascontiguousarray(X.reshape(N, 128, R)).astype(np.float32).astype(BF),
            "ha": np.stack([gtable(v) for v in a]), "hb": np.stack([gtable(v) for v in b]), "home": np.stack([gtable(v) for v in m]), "lo0": np.stack([gtable(v) for v in lo]), "hi0": np.stack([gtable(v) for v in hi])}
def setup_inputs(rng):
    return pack(*parts(rng))
def setup_inputs_ties(rng):
    Y, X, a, b, m, lo, hi = parts(rng)
    Y = np.take_along_axis(rng.integers(0, 256, (N, 8, 16, 4)), rng.integers(0, 4, (N, 8, 1, W)), 3)
    Y[:, 0] = Y[:, 0, :, :1]
    hi = np.where(rng.random(hi.shape) < 0.2, np.minimum(lo + rng.integers(0, E, hi.shape), W - 1), hi)
    m[:, :, :B] = (lo + hi) >> 1
    return pack(Y, X, a, b, m, lo, hi)
def setup_inputs_narrow(rng):
    Y, X, a, b, m, lo, hi = parts(rng)
    lo = rng.integers(0, W - 1, lo.shape); lo[:, :4] = rng.integers(0, W - 1024, (1, 4, 1)) + rng.integers(0, 40, (N, 4, B))
    hi = np.minimum(lo + rng.choice(np.array([0, 1, 2, E - 1, E, E + 1, 2 * E + 1, 300]), lo.shape), W - 1)
    for k, (p, q) in enumerate(((0, 0), (W - 1, W - 1), (0, W - 1), (W - 2, W - 1), (0, 1))): lo[:, 3:, k] = p; hi[:, 3:, k] = q
    t = rng.random((N, 5, R - B)) < 0.2
    a[:, 3:] = np.where(t, 1, a[:, 3:]); b[:, 3:] = np.where(t, H * R, b[:, 3:])
    lo[:, 7] = (E * np.arange(B)) % W; hi[:, 7] = np.minimum(lo[:, 7] + E, W - 1)
    o = np.arange(R - B); a[:, 7] = o; b[:, 7] = o + (o % B < B - 1)
    return pack(Y, X, a, b, m, lo, hi)
def setup_inputs_alike(rng):
    Y, X, a, b, m, lo, hi = parts(rng); lev = np.arange(B, R) // B
    v = a.reshape(N, 8, L - 1, B); a = np.where((np.arange(8) % 2 == 0)[None, :, None, None], v[..., :1], v).reshape(N, 8, R - B)
    a[:, 4] = rng.integers(0, H + 1, (N, 1)) * R + rng.integers(0, B, (N, 1))
    b[:, 1] = np.where(rng.random((N, R - B)) < 0.5, a[:, 1], b[:, 1]); b[:, 2] = a[:, 2]
    a[:, 3] = a[:, 3] % R; b[:, 3] = b[:, 3] % R
    a[:, 5] = a[:, 5] % R + H * R; b[:, 5] = b[:, 5] % R + H * R
    for w in (a, b): w[:, 7] = rng.integers(0, H + 1, (N, R - B)) * R + np.where(rng.random((N, R - B)) < 0.5, 0, B * lev - 1)
    return pack(Y, X, a, b, m, lo, hi)
def setup_inputs_far(rng):
    Y, X, a, b, m, lo, hi = parts(rng)
    Y = 255 * rng.integers(0, 2, Y.shape); X = 255 * rng.integers(0, 2, (N, 8, 1, R)) + np.zeros((1, 1, 16, 1), np.int64); m = (W - 1) * rng.integers(0, 2, m.shape)
    Y[:, 0] = 255; X[:, 0] = 0; Y[:, 1] = 0; X[:, 1] = 255; lo[:, :, :8] = 0; m[:, :, :4] = W - 1; m[:, :, 4:8] = 0
    for i, p, q, c in ((8, W - 1, W - 1, 0), (12, W - 16, W - 1, 0), (16, 0, 31, W - 1), (20, 1, 15, W - 1)): lo[:, :2, i:i + 4] = p; hi[:, :2, i:i + 4] = q; m[:, :2, i:i + 4] = c
    a[:, 1, ::B] = 8; b[:, 1, ::B] = H * R + 9
    Y[:, 2] = rng.integers(0, 2, (N, 16, W)); X[:, 2] = 255; hi[:, 2] = np.minimum(lo[:, 2] + 2 * E, W - 1)
    return pack(Y, X, a, b, m, lo, hi)
def setup_inputs_spread(rng):
    Y, X, a, b, m, lo, hi = parts(rng); lev = np.arange(B, R) // B
    Y = (np.exp2(rng.integers(1, 9, (N, 8, 1, W))) * rng.random(Y.shape)).astype(np.int64); X = (np.exp2(rng.integers(1, 9, (N, 8, 1, R))) * rng.random(X.shape)).astype(np.int64)
    a = (a // R) * R + (B * lev * rng.random(a.shape) ** 3).astype(np.int64); m = (W * rng.random(m.shape) ** 2).astype(np.int64)
    return pack(Y, X, a, b, m, lo, hi)
def check_inputs(d):
    bad = []
    for k in ("ytab", "xrow"):
        v = np.asarray(d[k]).astype(np.float32)
        if not np.all((v >= 0) & (v <= 255) & (v == np.floor(v))): bad.append("whole numbers of " + k)
    for k in ("home", "lo0", "hi0"):
        if np.min(d[k]) < 0 or np.max(d[k]) >= W: bad.append("range of " + k)
    if np.any(d["lo0"] > d["hi0"]): bad.append("lo0 over hi0")
    lev = np.arange(B, R) // B
    for k in ("ha", "hb"):
        h = np.stack([gentries(v) for v in d[k]]).astype(np.int64)
        if np.min(h) < 0 or np.max(h) >= (H + 1) * R or np.any(h % R >= B * lev): bad.append("rows that " + k + " names")
    return bad
def reference(ytab, xrow, ha, hb, home, lo0, hi0):
    Y = ytab.astype(np.float32).astype(np.int32).reshape(N, 8, 16, W); X = xrow.astype(np.float32).astype(np.int32).reshape(N, 8, 16, R)
    a, b, m, first, last = [np.stack([gentries(v) for v in t]).astype(np.int64) for t in (ha, hb, home, lo0, hi0)]
    e = np.arange(E); wins = []
    for ps in range(2):
        arg = np.zeros((N, 8, R), np.int64)
        for l in range(L):
            s = l * B
            if l == 0: lo, hi = first, last
            else:
                known = np.concatenate([np.roll(arg, -k, axis=0) for k in range(H + 1)], axis=2)
                u = np.take_along_axis(known, a[:, :, s - B:s], 2); v = np.take_along_axis(known, b[:, :, s - B:s], 2)
                lo, hi = np.minimum(u, v), np.maximum(u, v)
            j = lo[..., None] + (((hi - lo)[..., None] * e) >> SH)
            y = np.take_along_axis(Y, j.reshape(N, 8, 1, B * E), 3).reshape(N, 8, 16, B, E)
            cost = np.add.reduce(np.abs(X[..., s:s + B, None] - y), axis=2) + (np.abs(j - m[:, :, s:s + B, None]) >> 4)
            k = np.argmin(cost, axis=3)
            arg[:, :, s:s + B] = np.take_along_axis(j, k[..., None], 3)[..., 0]
        X = np.abs(X - np.take_along_axis(Y, arg[:, :, None, :], 3))
        wins.append(arg)
    both = np.concatenate(wins, axis=2)
    return {"argm": np.stack([gtable(v) for v in both]).astype(np.float32), "xo": X.reshape(N, 128, R).astype(np.float32)}

@@ -1,0 +1,451 @@
+import math
+from concourse.bass import DstId, RemoteDMATransfer
+from concourse.mybir import AluOpType as A, ActivationFunctionType as F
+
+RW = 4
+C0 = 31.0 / 64.0
+NB = 4
+
+MA = [("S3", 8), ("V2", 8), ("S3", 6), ("V2", 6), ("S3", 4)]
+MB = [("S3", 8), ("V2", 8), ("S3", 7), ("V2", 5), ("S3", 4)]
+PLAN = {
+    (0, 0): [("S3", 6), ("V2", 8), ("S3", 5), ("V2", 8), ("S3", 3), ("V2", 2)],
+    (1, 0): [("R3", 6), ("R3", 8), ("R3", 5), ("V2", 8), ("R3", 3), ("V2", 2)],
+    (0, 1): MA, (1, 1): MB, (0, 2): MA, (1, 2): MB, (0, 3): MA, (1, 3): MB,
+}
+COST = {"cyc": 0.00104, "gat": 1.56, "vfix": 0.06, "sfix": 0.08, "pe": 0.00052, "hop": 0.12, "same": 0.07,
+        "comm": 4.0, "comm0": 6.0, "yload": 6.0, "load": 2.2}
+CASES = [{}, {"gat": 1.2, "comm": 3.0, "comm0": 5.0, "yload": 5.0}, {"gat": 1.9, "comm": 5.0, "comm0": 7.0}]
+STEPS = 110000
+ORDER = {}
+
+BF16, F32, F16, I32, U16 = "bfloat16", "float32", "float16", "int32", "uint16"
+SCRATCH = {n: ("sbuf", [128, w], d) for n, w, d in [
+    ("Y", 4096, BF16), ("X0", 512, BF16), ("XR", 8 * RW * 128, BF16), ("GA", 16384, BF16), ("GB", 16384, BF16),
+    ("RA", 16384, BF16), ("RB", 16384, BF16), ("SM", 48, I32), ("HT", 288, I32), ("H4", 48, F32), ("HOFF", 48, U16),
+    ("ZH", 768, BF16), ("HM", 768, BF16), ("Z0", 768, F32), ("SF", 48, F32), ("BF", 8, F32), ("LT", 16, F32),
+    ("MT", 32, F32), ("T1", 128, I32), ("T2", 128, I32), ("MK", 128, BF16), ("DG", 16, F32), ("PM", 1, F32),
+    ("EI", 64, F32), ("EPS", 64, F32), ("C8", 8, U16), ("ONE", 128, BF16), ("ID", 128, BF16), ("NID", 128, BF16),
+    ("BO1", 128, BF16), ("BO", 128, BF16), ("BI", 8, BF16), ("W", 144, BF16), ("CS", 256, F32), ("KA", 128, I32),
+    ("KB", 128, I32), ("OFF", 2048, U16), ("WOFF", 64, U16), ("ZM", 2048, F16), ("AB", 2048, F32), ("HF", 2048, F16),
+    ("SC", 2048, F32), ("SP", 1024, F32), ("CI", 64, I32), ("EP", 64, F32), ("GM", 1024, BF16), ("DW", 1024, BF16),
+    ("XO", 512, F32), ("AM", 64, F32)]}
+SCRATCH["HH"] = ("sbuf", [128, 3, 2, 8], I32)
+SCRATCH.update({n: ("psum", [128, w], F32) for n, w in [("PA", 512), ("PB", 512), ("P0", 1024), ("P1", 1024), ("P2", 1024)]})
+DMAS = ["lo", "hi", "home", "ha", "hb", "x", "y", "xo0", "xo1", "xo2", "xo3", "am"]
+SEMAPHORES = (["qv", "qs", "qp", "qg", "sent"] + ["d_" + n for n in DMAS]
+              + ["arr%d%d" % (s, l) for s in range(2) for l in range(3)])
+
+
+def transfers_of(T, topo, r):
+    n = len(T.cores)
+    src = T.cores[r]
+    dsts = [(b, T.cores[(r - b) % n]) for b in range(1, NB)]
+    out, used = [], set()
+    for near in (False, True):
+        part = [d for d in dsts if (topo.chip(d[1]) == topo.chip(src)) == near]
+        if part:
+            es = set.intersection(*[set(topo.engines(src, c)) for _, c in part]) - used
+            used |= es
+            out.append((sum(1 << e for e in es), len(es), part))
+    return out
+
+
+def arrange(cases, nfirst):
+    ops = cases[0][0]
+    n = len(ops)
+    succ = [[] for _ in range(n)]
+    for i, o in enumerate(ops):
+        for d in o["deps"]:
+            succ[d].append(i)
+    eng = ["vspgy".index(o["eng"]) for o in ops]
+    tabs = []
+    for os_, c in cases:
+        gaps = [[(d, c["hop"] if eng[d] != eng[i] or os_[d]["kind"] != "c" else (0.0 if eng[i] == 2 else c["same"]))
+                 for d in o["deps"]] for i, o in enumerate(os_)]
+        tabs.append(([o["dur"] for o in os_], [o["lat"] for o in os_], gaps))
+
+    def span(seq):
+        tot = 0.0
+        for dur, lat, gaps in tabs:
+            free, fin = [0.0] * 5, [0.0] * n
+            for i in seq:
+                t = free[eng[i]]
+                for d, gp in gaps[i]:
+                    x = fin[d] + gp
+                    if x > t:
+                        t = x
+                t += dur[i]
+                free[eng[i]] = t
+                fin[i] = t + lat[i]
+            tot += max(fin)
+        return tot / len(tabs)
+
+    dur, lat, gaps = tabs[0]
+    togo = [0.0] * n
+    for i in range(n - 1, -1, -1):
+        togo[i] = dur[i] + lat[i] + max([togo[j] + 0.1 for j in succ[i]] + [0.0])
+    left = [len(o["deps"]) for o in ops]
+    free, fin, seq = [0.0] * 5, [0.0] * n, []
+    cand = {i: 0.0 for i in range(n) if not left[i]}
+    while cand:
+        i = min(cand, key=lambda j: (j >= nfirst, max(free[eng[j]], cand[j]), -togo[j]))
+        free[eng[i]] = max(free[eng[i]], cand.pop(i)) + dur[i]
+        fin[i] = free[eng[i]] + lat[i]
+        seq.append(i)
+        for j in succ[i]:
+            left[j] -= 1
+            if not left[j]:
+                cand[j] = max(fin[d] + gp for d, gp in gaps[j])
+    seq = list(range(nfirst)) + seq[nfirst:]
+    best = cur = span(seq)
+    now, x = seq, 12345
+    for it in range(STEPS):
+        x = (x * 6364136223846793005 + 1442695040888963407) % 18446744073709551616
+        p = nfirst + (x >> 40) % (n - nfirst)
+        i = now[p]
+        step = 1 if (x >> 30) & 1 else -1
+        hops = (1, 1, 1, 2, 3, 5, 1, 2)[(x >> 31) & 7]
+        bad = succ[i] if step > 0 else ops[i]["deps"]
+        q, to = p + step, None
+        while nfirst <= q < n and now[q] not in bad and hops:
+            if eng[now[q]] == eng[i]:
+                to, hops = q, hops - 1
+            q += step
+        if to is not None:
+            new = now[:p] + now[p + 1:]
+            new.insert(to, i)
+            val = span(new)
+            if val <= cur or ((x >> 8) & 65535) / 65536.0 < math.exp((cur - val) / (0.03 * (1 - it / STEPS) + 1e-4)):
+                cur, now = val, new
+                if val < best:
+                    best, seq = val, new
+    return seq, best
+
+
+def build(g, T, topo, rank, cost):
+    V, S, P = g.vector, g.scalar, g.tensor
+    ops, writer, readers = [], {}, {}
+    cyc, gat = cost["cyc"], cost["gat"]
+
+    def op(eng, dur, fn, reads, writes, kind="c", lat=0.0, sem=None, grp=None):
+        deps = {writer[k] for k in reads + writes if k in writer}
+        for k in writes:
+            deps |= set(readers.get(k, []))
+        i = len(ops)
+        for k in reads:
+            readers.setdefault(k, []).append(i)
+        for k in writes:
+            writer[k] = i
+            readers[k] = []
+        ops.append({"eng": eng, "dur": dur, "fn": fn, "deps": sorted(deps), "kind": kind, "lat": lat, "sem": sem,
+                    "grp": grp, "name": str((writes or reads)[0])})
+
+    def v(n, fn, reads, writes):
+        op("v", cost["vfix"] + n * cyc, lambda last: [fn()], reads, writes)
+
+    def vs(k, n, fn, reads, writes):
+        op("v", k * (cost["vfix"] + n * cyc), lambda last: [fn(j) for j in range(k)], reads, writes)
+
+    def s(n, fn, reads, writes):
+        op("s", cost["sfix"] + n * cyc, lambda last: [fn()], reads, writes)
+
+    def ss(k, n, fn, reads, writes):
+        op("s", k * (cost["sfix"] + n * cyc), lambda last: [fn(j) for j in range(k)], reads, writes)
+
+    def q(t, fn, reads, writes):
+        op("g", t, lambda last: [fn()], reads, writes)
+
+    def pe(n, fn, reads, writes, grp=None):
+        op("p", n * cost["pe"], fn, reads, writes, grp=grp)
+
+    def dma(eng, name, out, in_, reads, writes, lat):
+        qq = g.sync if eng == "y" else S
+        op(eng, 0.06, lambda last: qq.dma_start(out, in_), reads, writes, kind="d", lat=lat, sem="d_" + name)
+
+    ts, tt, cp, act, mm = V.tensor_scalar, V.tensor_tensor, V.tensor_copy, S.activation, P.matmul
+    dma("y", "lo", T.SM[:, 0:8], T.lo0[:], [], ["lo"], cost["load"])
+    dma("s", "hi", T.SM[:, 8:16], T.hi0[:], [], ["hi"], cost["load"])
+    dma("y", "home", T.SM[:, 16:48], T.home[:], [], ["home"], cost["load"])
+    dma("s", "x", T.X0[:], T.xrow[:], [], ["x"], cost["load"])
+    dma("y", "y", T.Y[:], T.ytab[:], [], ["y"], cost["yload"])
+    dma("y", "ha", T.HH[:, :, 0, :], T.ha[:], [], ["ha"], cost["yload"])
+    dma("y", "hb", T.HH[:, :, 1, :], T.hb[:], [], ["hb"], cost["yload"])
+
+    q(0.2, lambda: g.iota(T.EI[:, 0:32], [[1, 32]], 0, 0, allow_small_or_imprecise_dtypes=True), [], ["ei0"])
+    q(0.4, lambda: g.iota(T.T1[:], [[0, 8], [-1, 16]], 128, 1), [], ["t1"])
+    q(0.2, lambda: g.iota(T.EI[:, 32:64], [[-1, 32]], 31, 0, allow_small_or_imprecise_dtypes=True), [], ["ei1"])
+    v(64, lambda: V.memset(T.ONE[:], 1.0), [], ["one"])
+    q(0.45, lambda: g.affine_select(T.BO1[:], T.ONE[:], [[-16, 8], [0, 16]], A.is_ge, 0.0, 0, 1), ["one"], ["bo1"])
+    q(0.45, lambda: g.affine_select(T.BO[:], T.BO1[:], [[16, 8], [0, 16]], A.is_ge, 0.0, 15, -1), ["bo1"], ["bo"])
+    q(0.45, lambda: g.affine_select(T.ID[:], T.ONE[:], [[-1, 128]], A.is_equal, 0.0, 0, 1), ["one"], ["id"])
+    v(32, lambda: ts(T.EPS[:, 0:32], T.EI[:, 0:32], 1.0 / 32, None, A.mult), ["ei0"], ["eps0"])
+    v(32, lambda: ts(T.EPS[:, 32:64], T.EI[:, 32:64], 1.0 / 32, None, A.mult), ["ei1"], ["eps1"])
+    v(8, lambda: cp(T.C8[:], T.EI[:, 0:8]), ["ei0"], ["c8"])
+    v(128, lambda: ts(T.T2[:], T.T1[:], 15, None, A.bitwise_and), ["t1"], ["t2"])
+    v(16, lambda: ts(T.DG[:], T.T2[:, 0:16], 0.0, None, A.is_equal), ["t2"], ["dg"])
+    v(128, lambda: ts(T.MK[:], T.T2[:], 0.0, None, A.is_equal), ["t2"], ["mk"])
+    v(1, lambda: cp(T.PM[:], T.T2[:, 0:1]), ["t2"], ["pm"])
+    v(64, lambda: ts(T.NID[:], T.ID[:], -1.0, None, A.mult), ["id"], ["nid"])
+    v(8, lambda: cp(T.BI[:], T.BO[:, 0:128:16]), ["bo"], ["bi"])
+    v(72, lambda: V.memset(T.W[:], 0.0), [], ["w"])
+    v(8, lambda: cp(T.W[:, 15:128:16], T.BO[:, 0:128:16]), ["bo"], ["w"])
+    v(256, lambda: V.memset(T.CS[:], 1.0 / 32), [], ["cs"])
+    v(8, lambda: V.memset(T.CS[:, 0:256:32], 16384.0), [], ["cs"])
+
+    def xrc(u, c0, c1):
+        return T.XR[:, u * RW * 128 + c0:u * RW * 128 + c1]
+
+    def copy(on_s, o, i_, n, ks, kw):
+        if on_s:
+            s(n, lambda: act(o, i_, F.Copy), ks, kw)
+        else:
+            v(n / 2, lambda: cp(o, i_), ks, kw)
+
+    def widen(u, h, on_s):
+        while h < RW:
+            copy(on_s, xrc(u, h * 128, 2 * h * 128), xrc(u, 0, h * 128), h * 128, [("xr", u, j) for j in range(h)],
+                 [("xr", u, j) for j in range(h, 2 * h)])
+            h *= 2
+
+    def rows_pass1(l):
+        for j in range(2):
+            copy(l != 0, xrc(l, j * 128, (j + 1) * 128), T.X0[:, l * 128:(l + 1) * 128], 128, ["x"], [("xr", l, j)])
+        widen(l, 2, l != 0)
+
+    def sp(u, c0, c1, st=1):
+        return T.SP[:, u * 128 + c0:u * 128 + c1:st]
+
+    def offsets_and_home(u, dl, lol, dt_, bt, st, kl, kt):
+        def col(c):
+            return sp(u, c, c + 1)
+        vs(8, 32, lambda j: ts(T.OFF[:, u * 256 + j:(u + 1) * 256:8], T.EPS[:, 0:32], col(dl + st * j), col(lol + st * j),
+                               A.mult, A.add), kl + ["eps0"], [("off", u)])
+        ss(8, 32, lambda j: act(T.AB[:, u * 256 + j * 32:u * 256 + (j + 1) * 32], T.EPS[:, 32:64], F.Abs,
+                                bias=col(bt + j), scale=col(dt_ + st * j)), kt + ["eps1"], [("ab", u)])
+        v(256, lambda: ts(T.HF[:, u * 256:(u + 1) * 256], T.AB[:, u * 256:(u + 1) * 256], 1.0 / 16, 1535.53125,
+                          A.mult, A.add), [("ab", u)], [("hf", u)])
+
+    v(8, lambda: ts(sp(0, 32, 40), T.SM[:, 0:8], -C0, None, A.add), ["lo"], [("lo", 0)])
+    v(16, lambda: tt(sp(0, 64, 72), T.SM[:, 8:16], T.SM[:, 0:8], A.subtract), ["lo", "hi"], [("d", 0)])
+    v(8, lambda: ts(sp(0, 88, 96), T.SM[:, 0:8], -C0 - 2048.0, None, A.add), ["lo"], [("loc", 0)])
+    v(48, lambda: cp(T.SF[:], T.SM[:]), ["lo", "hi", "home"], ["sf"])
+    v(8, lambda: cp(T.BF[:], T.BO[:, 0:128:16]), ["bo"], ["bf"])
+    ss(9, 48, lambda k: act(T.Z0[:, k:768:16], T.SF[:], F.Identity, scale=T.DG[:, k:k + 1]), ["sf", "dg"], ["z0"])
+    vs(7, 48, lambda k: ts(T.Z0[:, k + 9:768:16], T.SF[:], T.DG[:, k + 9:k + 10], None, A.mult), ["sf", "dg"], ["z1"])
+    pe(24 * 64, lambda last: [mm(T.P1[:, j * 8:(j + 1) * 8], T.Z0[:, j * 128:(j + 1) * 128], T.BF[:], True, True)
+                              for j in range(6)], ["z0", "z1", "bf"], [("ps", 1)])
+    v(16, lambda: ts(T.LT[:], T.P1[:, 0:16], -C0, None, A.add), [("ps", 1)], ["lt"])
+    v(32, lambda: cp(T.MT[:], T.P1[:, 16:48]), [("ps", 1)], ["mt"])
+    v(16, lambda: tt(sp(0, 72, 80), T.LT[:, 8:16], T.LT[:, 0:8], A.subtract), ["lt"], [("dt", 0)])
+    v(16, lambda: tt(sp(0, 80, 88), T.LT[:, 0:8], T.MT[:, 0:8], A.subtract), ["lt", "mt"], [("bt", 0)])
+    offsets_and_home(0, 64, 32, 72, 80, 1, [("lo", 0), ("d", 0)], [("dt", 0), ("bt", 0)])
+    rows_pass1(0)
+
+    def hints():
+        def ht(j):
+            return T.HT[:, j * 48:(j + 1) * 48]
+        hk = ["ha", "hb", ("sc", 0)]
+        v(48, lambda: ts(ht(5), T.HH[:], 15, None, A.bitwise_and), hk, ["h5"])
+        v(48, lambda: cp(T.H4[:], ht(5)), ["h5"], ["h4f"])
+        v(48, lambda: ts(ht(0), T.HH[:], 2, 0x60, A.logical_shift_right, A.bitwise_and), hk, ["h0"])
+        v(48, lambda: ts(ht(1), T.HH[:], 6, 0x18, A.logical_shift_right, A.bitwise_and), hk, ["h1"])
+        v(48, lambda: ts(ht(2), T.HH[:], 4, 7, A.logical_shift_right, A.bitwise_and), hk, ["h2"])
+        v(96, lambda: tt(ht(3), ht(0), ht(1), A.add), ["h0", "h1"], ["h3"])
+        v(96, lambda: tt(ht(4), ht(3), ht(2), A.add), ["h3", "h2"], ["h4"])
+        v(48, lambda: cp(T.HOFF[:], ht(4)), ["h4"], ["hoff"])
+        ss(16, 48, lambda k: act(T.ZH[:, k:768:16], T.H4[:], F.Identity, scale=T.DG[:, k:k + 1]), ["h4f", "dg"], ["zh"])
+        pe(768, lambda last: [mm(T.P0[:, 0:512], T.BO[:], T.ZH[:, 0:512], True, True),
+                              mm(T.P0[:, 512:768], T.BO[:], T.ZH[:, 512:768], True, True)], ["zh", "bo"], [("ps", 0)])
+        v(768, lambda: ts(T.HM[:], T.P0[:, 0:768], T.PM[:], None, A.is_equal), [("ps", 0), "pm"], ["hm"])
+        for l in range(1, 4):
+            rows_pass1(l)
+
+    plan = transfers_of(T, topo, rank)
+    slot = [2]
+    held = {}
+    PS = [T.P0, T.P1, T.P2]
+
+    def unit(ps, l):
+        u = ps * 4 + l
+        ub = 0 if l == 0 else u
+        K, KEY, G, R = (T.KB, T.PB, T.GB, T.RB) if ps else (T.KA, T.PA, T.GA, T.RA)
+        bank = ("key", ps)
+        if l > 0:
+            zm = T.ZM[:, u * 256:(u + 1) * 256]
+            v(256 * gat, lambda: tt(zm, K[:, 0:32 * l].indirect(T.HOFF[:, 16 * (l - 1):16 * l]),
+                                    T.HM[:, 256 * (l - 1):256 * l], A.mult),
+              ["hoff", "hm"] + [("k", ps, j) for j in range(l)] + [("arr", ps, j) for j in range(l)], [("zm", u)])
+
+            def ends(last):
+                r = [mm(KEY[:, 256:288:2], T.W[:, 15 - k:143 - k], T.ZM[:, u * 256 + k:(u + 1) * 256:16], k == 0, k == 15)
+                     for k in range(16)]
+                r.append(mm(KEY[:, 257:272:2], T.ZM[:, u * 256:u * 256 + 128], T.BI[:], True, True))
+                r.append(mm(KEY[:, 273:288:2], T.ZM[:, u * 256 + 128:(u + 1) * 256], T.BI[:], True, True))
+                return r
+            pe(18 * 64, ends, [("zm", u), "w", "bi"], [bank])
+            v(32, lambda: ts(sp(u, 0, 32), KEY[:, 256:288], 2048.0 - C0, None, A.add), [bank], [("uv", u)])
+            v(32, lambda: tt(sp(u, 32, 48), sp(u, 0, 16), sp(u, 16, 32), A.min), [("uv", u)], [("lo", u)])
+            v(32, lambda: tt(sp(u, 48, 64), sp(u, 0, 16), sp(u, 16, 32), A.max), [("uv", u)], [("hi", u)])
+            v(32, lambda: tt(sp(u, 64, 80), sp(u, 48, 64), sp(u, 32, 48), A.subtract), [("lo", u), ("hi", u)], [("d", u)])
+            v(16, lambda: tt(sp(u, 80, 88), sp(u, 33, 48, 2), T.MT[:, 8 * l:8 * l + 8], A.subtract), [("lo", u), "mt"], [("bt", u)])
+            s(8, lambda: act(sp(u, 88, 96), sp(u, 32, 48, 2), F.Identity, bias=-2048.0), [("lo", u)], [("loc", u)])
+            offsets_and_home(u, 64, 32, 65, 80, 2, [("lo", u), ("d", u)], [("d", u), ("bt", u)])
+        dlist = sp(0, 64, 72) if l == 0 else sp(u, 64, 80, 2)
+        pe(256, lambda last: [mm(KEY[:, 0:256], T.ID[:], T.HF[:, ub * 256:(ub + 1) * 256], True, False)],
+           [("hf", ub), "id"], [bank])
+        xk = [("xr", u, j) for j in range(RW)]
+
+        def sums(terms, e0, e1, reads):
+            def fn(last):
+                todo = [(e, t) for e in range(e0, e1) for t in terms]
+                return [mm(KEY[:, 31 - e:256:32], t[:, l * 4096 + e * 128:l * 4096 + (e + 1) * 128], T.BI[:],
+                           False, last and j == len(todo) - 1) for j, (e, t) in enumerate(todo)]
+            pe(64 * len(terms) * (e1 - e0), fn, reads + [bank, "bi"], [], grp=u)
+
+        def items(h, h1):
+            return T.Y[:, 0:4096].indirect(T.OFF[:, ub * 256 + h * 8:ub * 256 + h1 * 8])
+
+        def piece(kind, e0, e1):
+            n = (e1 - e0) * 128
+            c0 = l * 4096 + e0 * 128
+            src, r_ = G, R[:, c0:c0 + n]
+            gk, rk = [("g", u, e0)], ("r", u, e0)
+            if kind in ("V1", "V2"):
+                def one(h, h1):
+                    v((h1 - h) * 128 * gat, lambda: tt(G[:, l * 4096 + h * 128:l * 4096 + h1 * 128], items(h, h1),
+                                                       xrc(u, 0, (h1 - h) * 128), A.subtract),
+                      ["y", ("off", ub)] + xk[:h1 - h], [("g", u, h)])
+                for h in range(e0, e1, RW):
+                    one(h, min(e1, h + RW))
+                gk = [("g", u, h) for h in range(e0, e1, RW)]
+                held[(u, e0)] = "D"
+                if kind == "V2":
+                    v(n / 2, lambda: ts(r_, G[:, c0:c0 + n], 0.0, -2.0, A.min, A.mult), gk, [rk])
+                    sums([G, R], e0, e1, gk + [rk])
+                else:
+                    s(n, lambda: act(r_, G[:, c0:c0 + n], F.Abs), gk, [rk])
+                    sums([R], e0, e1, [rk])
+                return
+            back = False
+            if kind == "S3":
+                s(n * gat, lambda: act(G[:, c0:c0 + n], items(e0, e1), F.Copy), ["y", ("off", ub)], gk)
+                held[(u, e0)] = "G"
+            else:
+                src, gk = T.GA, [("g", 0, h) for h in range(e0, e1)]
+                back = held[(0, e0)] == "D"
+            sl = slot[0] % 3
+            slot[0] += 1
+            pk = ("ps", sl)
+
+            def diff(last):
+                r = []
+                for h in range(0, n, 512):
+                    m = min(512, n - h)
+                    r.append(mm(PS[sl][:, h:h + m], T.ID[:], src[:, c0 + h:c0 + h + m], True, False))
+                    if back:
+                        r.append(mm(PS[sl][:, h:h + m], T.ID[:], xrc(0, 0, m), False, False))
+                    st = 128 if ps else m
+                    for c in range(0, m, st):
+                        r.append(mm(PS[sl][:, h + c:h + c + st], T.NID[:], xrc(u, 0, st), False, c + st == m))
+                return r
+            pe(n * (3 if back else 2), diff, gk + ["id", "nid"] + (xk[:1] if ps else xk[:4])
+               + ([("xr", 0, j) for j in range(4)] if back else []), [pk])
+            s(n, lambda: act(r_, PS[sl][:, 0:n], F.Abs), [pk], [rk])
+            sums([R], e0, e1, [rk])
+
+        e = 0
+        for kind, ne in PLAN[(ps, l)]:
+            piece(kind, e, e + ne)
+            e += ne
+
+        fin = T.SC[:, u * 256 + 31:(u + 1) * 256:32]
+        ci, ep = T.CI[:, u * 8:u * 8 + 8], T.EP[:, u * 8:u * 8 + 8]
+        gm, dw = T.GM[:, u * 128:(u + 1) * 128], T.DW[:, u * 128:(u + 1) * 128]
+        own = K[:, 32 * l:32 * l + 8]
+        wo = T.WOFF[:, u * 8:u * 8 + 8]
+        v(256, lambda: V.tensor_tensor_scan(T.SC[:, u * 256:(u + 1) * 256], T.CS[:], KEY[:, 0:256], 0.0, A.add, A.min),
+          ["cs"], [("sc", u), bank])
+        v(8, lambda: ts(ci, fin, -C0, None, A.add), [("sc", u)], [("ci", u)])
+        v(16, lambda: tt(ep, fin, ci, A.subtract), [("sc", u), ("ci", u)], [("ep", u)])
+        v(128 * gat, lambda: tt(gm, ep.indirect(T.C8[:]), T.MK[:], A.mult), [("ep", u), "c8", "mk"], [("gm", u)])
+        pe(64, lambda last: [mm(KEY[:, 288:296], gm, T.BI[:], True, True)], [("gm", u), "bi"], [bank])
+        v(8, lambda: tt(sp(u, 96, 104), KEY[:, 288:296], dlist, A.mult), [bank, ("d", ub)], [("ed", u)])
+        v(16, lambda: tt(own, sp(u, 96, 104), sp(ub, 88, 96), A.add), [("ed", u), ("loc", ub)], [("k", ps, l)])
+        if l < 3:
+            def send(last):
+                return g.remote_dma_fused([RemoteDMATransfer(
+                    dst_ids=[DstId(rid=topo.addr(c)[0], pnc=topo.addr(c)[1]) for _, c in part],
+                    dma_engine_mask=mask, remote_sem=T.sem["arr%d%d" % (ps, l)], srcs=[own],
+                    dsts=[K[:, 32 * l + 8 * b:32 * l + 8 * b + 8] for b, _ in part]) for mask, _, part in plan],
+                    local_sem=T.sem.sent)
+            op("g", 0.3, send, [("k", ps, l)], [("arr", ps, l)], kind="r",
+               lat=cost["comm0"] if u == 0 else cost["comm"], sem="arr%d%d" % (ps, l))
+        v(8, lambda: ts(wo, own, 2048.0, None, A.add), [("k", ps, l)], [("wo", u)])
+        v(128 * gat, lambda: tt(dw, T.Y[:, 0:4096].indirect(wo), xrc(u, 0, 128), A.subtract), ["y", ("wo", u), xk[0]], [("dw", u)])
+        if ps == 0:
+            v(64, lambda: ts(gm, dw, 0.0, -2.0, A.min, A.mult), [("dw", u)], [("gm", u)])
+            v(128, lambda: tt(xrc(u + 4, 0, 128), dw, gm, A.add), [("dw", u), ("gm", u)], [("xr", u + 4, 0)])
+            widen(u + 4, 1, False)
+        else:
+            xo = T.XO[:, l * 128:(l + 1) * 128]
+            s(128, lambda: act(xo, dw, F.Abs), [("dw", u)], [("xo", l)])
+            dma("s" if l == 3 else "y", "xo%d" % l, T.xo[:, l * 128:(l + 1) * 128], xo, [("xo", l)], [], cost["load"])
+
+    for l in range(4):
+        unit(0, l)
+        if l == 0:
+            hints()
+        unit(1, l)
+    v(64, lambda: cp(T.AM[:], T.WOFF[:]), [("wo", u) for u in range(8)], ["am"])
+    dma("y", "am", T.argm[:], T.AM[:], ["am"], [], cost["load"])
+    return ops, list(range(7)), plan
+
+
+def rank_program(g, core, T, topo):
+    rank = T.rank_of(core)
+    if rank is None:
+        return
+    ops, first, plan = build(g, T, topo, rank, COST)
+    if not ORDER:
+        cases = [dict(COST, **c) for c in CASES]
+        ORDER["seq"], ORDER["span"] = arrange([(build(g, T, topo, rank, c)[0], c) for c in cases], len(first))
+    seq = ORDER["seq"]
+    arrive = sum(k for b in range(1, NB) for _, k, part in transfers_of(T, topo, (rank + b) % len(T.cores))
+                 for _, c in part if c == core)
+    queue = {"v": g.vector, "s": g.scalar, "p": g.tensor, "g": g, "y": g.sync}
+    lastof = {ops[i]["grp"]: i for i in seq}
+    count = {"qv": 0, "qs": 0, "qp": 0, "qg": 0}
+    seen = {e: {} for e in queue}
+    done = {}
+    sent = 0
+    for i in seq:
+        o = ops[i]
+        e = o["eng"]
+        know = seen[e]
+        for d in sorted(o["deps"], key=lambda j: -done[j][1]):
+            sem, val, with_it = done[d]
+            if (e == "p" and sem == "qp") or know.get(sem, 0) >= val:
+                continue
+            queue[e].wait_ge(T.sem[sem], val)
+            for k2, v2 in with_it.items():
+                know[k2] = max(know.get(k2, 0), v2)
+            know[sem] = val
+        r = o["fn"](lastof[o["grp"]] == i)
+        if o["kind"] == "c":
+            sem = "q" + e
+            for ins in r:
+                ins.then_inc(T.sem[sem], 1)
+            count[sem] += len(r)
+            done[i] = (sem, count[sem], dict(know))
+        elif o["kind"] == "d":
+            r.then_inc(T.sem[o["sem"]], 16)
+            done[i] = (o["sem"], 16, dict(know))
+        else:
+            sent += sum(k for _, k, _ in plan)
+            done[i] = (o["sem"], arrive, {})
+    g.wait_ge(T.sem.sent, sent)
+    for sem, val in count.items():
+        g.sync.wait_ge(T.sem[sem], val)
+    for nme in DMAS:
+        g.sync.wait_ge(T.sem["d_" + nme], 16)

@@ -5,18 +5,23 @@ from concourse.mybir import AluOpType as A, ActivationFunctionType as F
 RW = 4
 C0 = 31.0 / 64.0
 NB = 4
-
-MA = [("S3", 8), ("V2", 8), ("S3", 6), ("V2", 6), ("S3", 4)]
-MB = [("S3", 8), ("V2", 8), ("S3", 7), ("V2", 5), ("S3", 4)]
+MA = [("S3", 8), ("V2", 8), ("S3", 5), ("V2", 7), ("S3", 4)]
+MB = [("S3", 8), ("V2", 8), ("S3", 6), ("V2", 6), ("S3", 4)]
 PLAN = {
     (0, 0): [("S3", 6), ("V2", 8), ("S3", 5), ("V2", 8), ("S3", 3), ("V2", 2)],
     (1, 0): [("R3", 6), ("R3", 8), ("R3", 5), ("V2", 8), ("R3", 3), ("V2", 2)],
     (0, 1): MA, (1, 1): MB, (0, 2): MA, (1, 2): MB, (0, 3): MA, (1, 3): MB,
 }
-COST = {"cyc": 0.00104, "gat": 1.56, "vfix": 0.06, "sfix": 0.08, "pe": 0.00052, "hop": 0.12, "same": 0.07,
-        "comm": 4.0, "comm0": 6.0, "yload": 6.0, "load": 2.2}
-CASES = [{}, {"gat": 1.2, "comm": 3.0, "comm0": 5.0, "yload": 5.0}, {"gat": 1.9, "comm": 5.0, "comm0": 7.0}]
-STEPS = 110000
+
+
+def case(f, gat, comm, fix, hop):
+    return {"cyc": 0.00083 * f, "gat": gat, "vfix": fix * f, "sfix": (fix + 0.015) * f, "pe": 0.42 * f / 1000,
+            "hop": hop, "same": hop * 0.6, "comm": comm, "comm0": comm + 0.5, "yload": 5.5, "load": 2.2}
+
+
+CASES = [case(1.0, 1.56, 3.7, 0.05, 0.2), case(1.3, 1.8, 3.7, 0.05, 0.2)]
+COST = CASES[0]
+STEPS = 220000
 ORDER = {}
 
 BF16, F32, F16, I32, U16 = "bfloat16", "float32", "float16", "int32", "uint16"
@@ -116,7 +121,7 @@ def arrange(cases, nfirst):
             new = now[:p] + now[p + 1:]
             new.insert(to, i)
             val = span(new)
-            if val <= cur or ((x >> 8) & 65535) / 65536.0 < math.exp((cur - val) / (0.03 * (1 - it / STEPS) + 1e-4)):
+            if val <= cur or ((x >> 8) & 65535) / 65536.0 < math.exp((cur - val) / (0.06 * (1 - it / STEPS) + 1e-4)):
                 cur, now = val, new
                 if val < best:
                     best, seq = val, new
@@ -138,8 +143,7 @@ def build(g, T, topo, rank, cost):
         for k in writes:
             writer[k] = i
             readers[k] = []
-        ops.append({"eng": eng, "dur": dur, "fn": fn, "deps": sorted(deps), "kind": kind, "lat": lat, "sem": sem,
-                    "grp": grp, "name": str((writes or reads)[0])})
+        ops.append({"eng": eng, "dur": dur, "fn": fn, "deps": sorted(deps), "kind": kind, "lat": lat, "sem": sem, "grp": grp})
 
     def v(n, fn, reads, writes):
         op("v", cost["vfix"] + n * cyc, lambda last: [fn()], reads, writes)
@@ -162,6 +166,14 @@ def build(g, T, topo, rank, cost):
     def dma(eng, name, out, in_, reads, writes, lat):
         qq = g.sync if eng == "y" else S
         op(eng, 0.06, lambda last: qq.dma_start(out, in_), reads, writes, kind="d", lat=lat, sem="d_" + name)
+
+    plan = transfers_of(T, topo, rank)
+
+    def send(src, dst, sem, reads, key, lat):
+        op("g", 0.3, lambda last: g.remote_dma_fused([RemoteDMATransfer(
+            dst_ids=[DstId(rid=topo.addr(c)[0], pnc=topo.addr(c)[1]) for _, c in part], dma_engine_mask=mask,
+            remote_sem=T.sem[sem], srcs=[src], dsts=[dst(b) for b, _ in part]) for mask, _, part in plan],
+            local_sem=T.sem.sent), reads, [key], kind="r", lat=lat, sem=sem)
 
     ts, tt, cp, act, mm = V.tensor_scalar, V.tensor_tensor, V.tensor_copy, S.activation, P.matmul
     dma("y", "lo", T.SM[:, 0:8], T.lo0[:], [], ["lo"], cost["load"])
@@ -228,7 +240,7 @@ def build(g, T, topo, rank, cost):
 
     v(8, lambda: ts(sp(0, 32, 40), T.SM[:, 0:8], -C0, None, A.add), ["lo"], [("lo", 0)])
     v(16, lambda: tt(sp(0, 64, 72), T.SM[:, 8:16], T.SM[:, 0:8], A.subtract), ["lo", "hi"], [("d", 0)])
-    v(8, lambda: ts(sp(0, 88, 96), T.SM[:, 0:8], -C0 - 2048.0, None, A.add), ["lo"], [("loc", 0)])
+    v(8, lambda: ts(sp(0, 72, 80), T.SM[:, 0:8], -C0 - 2048.0, None, A.add), ["lo"], [("loc", 0)])
     v(48, lambda: cp(T.SF[:], T.SM[:]), ["lo", "hi", "home"], ["sf"])
     v(8, lambda: cp(T.BF[:], T.BO[:, 0:128:16]), ["bo"], ["bf"])
     ss(9, 48, lambda k: act(T.Z0[:, k:768:16], T.SF[:], F.Identity, scale=T.DG[:, k:k + 1]), ["sf", "dg"], ["z0"])
@@ -237,9 +249,9 @@ def build(g, T, topo, rank, cost):
                               for j in range(6)], ["z0", "z1", "bf"], [("ps", 1)])
     v(16, lambda: ts(T.LT[:], T.P1[:, 0:16], -C0, None, A.add), [("ps", 1)], ["lt"])
     v(32, lambda: cp(T.MT[:], T.P1[:, 16:48]), [("ps", 1)], ["mt"])
-    v(16, lambda: tt(sp(0, 72, 80), T.LT[:, 8:16], T.LT[:, 0:8], A.subtract), ["lt"], [("dt", 0)])
+    v(16, lambda: tt(sp(0, 88, 96), T.LT[:, 8:16], T.LT[:, 0:8], A.subtract), ["lt"], [("dt", 0)])
     v(16, lambda: tt(sp(0, 80, 88), T.LT[:, 0:8], T.MT[:, 0:8], A.subtract), ["lt", "mt"], [("bt", 0)])
-    offsets_and_home(0, 64, 32, 72, 80, 1, [("lo", 0), ("d", 0)], [("dt", 0), ("bt", 0)])
+    offsets_and_home(0, 64, 32, 88, 80, 1, [("lo", 0), ("d", 0)], [("dt", 0), ("bt", 0)])
     rows_pass1(0)
 
     def hints():
@@ -261,7 +273,6 @@ def build(g, T, topo, rank, cost):
         for l in range(1, 4):
             rows_pass1(l)
 
-    plan = transfers_of(T, topo, rank)
     slot = [2]
     held = {}
     PS = [T.P0, T.P1, T.P2]
@@ -311,7 +322,7 @@ def build(g, T, topo, rank, cost):
             c0 = l * 4096 + e0 * 128
             src, r_ = G, R[:, c0:c0 + n]
             gk, rk = [("g", u, e0)], ("r", u, e0)
-            if kind in ("V1", "V2"):
+            if kind == "V2":
                 def one(h, h1):
                     v((h1 - h) * 128 * gat, lambda: tt(G[:, l * 4096 + h * 128:l * 4096 + h1 * 128], items(h, h1),
                                                        xrc(u, 0, (h1 - h) * 128), A.subtract),
@@ -320,12 +331,8 @@ def build(g, T, topo, rank, cost):
                     one(h, min(e1, h + RW))
                 gk = [("g", u, h) for h in range(e0, e1, RW)]
                 held[(u, e0)] = "D"
-                if kind == "V2":
-                    v(n / 2, lambda: ts(r_, G[:, c0:c0 + n], 0.0, -2.0, A.min, A.mult), gk, [rk])
-                    sums([G, R], e0, e1, gk + [rk])
-                else:
-                    s(n, lambda: act(r_, G[:, c0:c0 + n], F.Abs), gk, [rk])
-                    sums([R], e0, e1, [rk])
+                v(n / 2, lambda: ts(r_, G[:, c0:c0 + n], 0.0, -2.0, A.min, A.mult), gk, [rk])
+                sums([G, R], e0, e1, gk + [rk])
                 return
             back = False
             if kind == "S3":
@@ -371,22 +378,19 @@ def build(g, T, topo, rank, cost):
         v(128 * gat, lambda: tt(gm, ep.indirect(T.C8[:]), T.MK[:], A.mult), [("ep", u), "c8", "mk"], [("gm", u)])
         pe(64, lambda last: [mm(KEY[:, 288:296], gm, T.BI[:], True, True)], [("gm", u), "bi"], [bank])
         v(8, lambda: tt(sp(u, 96, 104), KEY[:, 288:296], dlist, A.mult), [bank, ("d", ub)], [("ed", u)])
-        v(16, lambda: tt(own, sp(u, 96, 104), sp(ub, 88, 96), A.add), [("ed", u), ("loc", ub)], [("k", ps, l)])
+        v(16, lambda: tt(own, sp(u, 96, 104), sp(0, 72, 80) if l == 0 else sp(u, 88, 96), A.add),
+          [("ed", u), ("loc", ub)], [("k", ps, l)])
         if l < 3:
-            def send(last):
-                return g.remote_dma_fused([RemoteDMATransfer(
-                    dst_ids=[DstId(rid=topo.addr(c)[0], pnc=topo.addr(c)[1]) for _, c in part],
-                    dma_engine_mask=mask, remote_sem=T.sem["arr%d%d" % (ps, l)], srcs=[own],
-                    dsts=[K[:, 32 * l + 8 * b:32 * l + 8 * b + 8] for b, _ in part]) for mask, _, part in plan],
-                    local_sem=T.sem.sent)
-            op("g", 0.3, send, [("k", ps, l)], [("arr", ps, l)], kind="r",
-               lat=cost["comm0"] if u == 0 else cost["comm"], sem="arr%d%d" % (ps, l))
+            send(own, lambda b: K[:, 32 * l + 8 * b:32 * l + 8 * b + 8], "arr%d%d" % (ps, l), [("k", ps, l)],
+                 ("arr", ps, l), cost["comm"] if u else cost["comm0"])
         v(8, lambda: ts(wo, own, 2048.0, None, A.add), [("k", ps, l)], [("wo", u)])
-        v(128 * gat, lambda: tt(dw, T.Y[:, 0:4096].indirect(wo), xrc(u, 0, 128), A.subtract), ["y", ("wo", u), xk[0]], [("dw", u)])
+        v(128 * gat, lambda: tt(dw, T.Y[:, 0:4096].indirect(wo), xrc(u, 0, 128), A.subtract),
+          ["y", ("wo", u), xk[0]], [("dw", u)])
         if ps == 0:
             v(64, lambda: ts(gm, dw, 0.0, -2.0, A.min, A.mult), [("dw", u)], [("gm", u)])
             v(128, lambda: tt(xrc(u + 4, 0, 128), dw, gm, A.add), [("dw", u), ("gm", u)], [("xr", u + 4, 0)])
-            widen(u + 4, 1, False)
+            v(128, lambda: tt(xrc(u + 4, 128, 256), dw, gm, A.add), [("dw", u), ("gm", u)], [("xr", u + 4, 1)])
+            widen(u + 4, 2, False)
         else:
             xo = T.XO[:, l * 128:(l + 1) * 128]
             s(128, lambda: act(xo, dw, F.Abs), [("dw", u)], [("xo", l)])
@@ -408,8 +412,7 @@ def rank_program(g, core, T, topo):
         return
     ops, first, plan = build(g, T, topo, rank, COST)
     if not ORDER:
-        cases = [dict(COST, **c) for c in CASES]
-        ORDER["seq"], ORDER["span"] = arrange([(build(g, T, topo, rank, c)[0], c) for c in cases], len(first))
+        ORDER["seq"], ORDER["span"] = arrange([(build(g, T, topo, rank, c)[0], c) for c in CASES], len(first))
     seq = ORDER["seq"]
     arrive = sum(k for b in range(1, NB) for _, k, part in transfers_of(T, topo, (rank + b) % len(T.cores))
                  for _, c in part if c == core)

import math
from concourse.bass import DstId, RemoteDMATransfer
from concourse.mybir import AluOpType as A, ActivationFunctionType as F

RW = 4
C0 = 31.0 / 64.0
NB = 4
MA = [("S3", 8), ("V2", 8), ("S3", 5), ("V2", 7), ("S3", 4)]
MB = [("S3", 8), ("V2", 8), ("S3", 6), ("V2", 6), ("S3", 4)]
PLAN = {
    (0, 0): [("S3", 6), ("V2", 8), ("S3", 5), ("V2", 8), ("S3", 3), ("V2", 2)],
    (1, 0): [("R3", 6), ("R3", 8), ("R3", 5), ("V2", 8), ("R3", 3), ("V2", 2)],
    (0, 1): MA, (1, 1): MB, (0, 2): MA, (1, 2): MB, (0, 3): MA, (1, 3): MB,
}


def case(f, gat, comm, fix, hop):
    return {"cyc": 0.00083 * f, "gat": gat, "vfix": fix * f, "sfix": (fix + 0.015) * f, "pe": 0.42 * f / 1000,
            "hop": hop, "same": hop * 0.6, "comm": comm, "comm0": comm + 0.5, "yload": 5.5, "load": 2.2}


CASES = [case(1.0, 1.56, 3.7, 0.05, 0.2), case(1.3, 1.8, 3.7, 0.05, 0.2)]
COST = CASES[0]
STEPS = 220000
ORDER = {}

BF16, F32, F16, I32, U16 = "bfloat16", "float32", "float16", "int32", "uint16"
SCRATCH = {n: ("sbuf", [128, w], d) for n, w, d in [
    ("Y", 4096, BF16), ("X0", 512, BF16), ("XR", 8 * RW * 128, BF16), ("GA", 16384, BF16), ("GB", 16384, BF16),
    ("RA", 16384, BF16), ("RB", 16384, BF16), ("SM", 48, I32), ("HT", 288, I32), ("H4", 48, F32), ("HOFF", 48, U16),
    ("ZH", 768, BF16), ("HM", 768, BF16), ("Z0", 768, F32), ("SF", 48, F32), ("BF", 8, F32), ("LT", 16, F32),
    ("MT", 32, F32), ("T1", 128, I32), ("T2", 128, I32), ("MK", 128, BF16), ("DG", 16, F32), ("PM", 1, F32),
    ("EI", 64, F32), ("EPS", 64, F32), ("C8", 8, U16), ("ONE", 128, BF16), ("ID", 128, BF16), ("NID", 128, BF16),
    ("BO1", 128, BF16), ("BO", 128, BF16), ("BI", 8, BF16), ("W", 144, BF16), ("CS", 256, F32), ("KA", 128, I32),
    ("KB", 128, I32), ("OFF", 2048, U16), ("WOFF", 64, U16), ("ZM", 2048, F16), ("AB", 2048, F32), ("HF", 2048, F16),
    ("SC", 2048, F32), ("SP", 1024, F32), ("CI", 64, I32), ("EP", 64, F32), ("GM", 1024, BF16), ("DW", 1024, BF16),
    ("XO", 512, F32), ("AM", 64, F32)]}
SCRATCH["HH"] = ("sbuf", [128, 3, 2, 8], I32)
SCRATCH.update({n: ("psum", [128, w], F32) for n, w in [("PA", 512), ("PB", 512), ("P0", 1024), ("P1", 1024), ("P2", 1024)]})
DMAS = ["lo", "hi", "home", "ha", "hb", "x", "y", "xo0", "xo1", "xo2", "xo3", "am"]
SEMAPHORES = (["qv", "qs", "qp", "qg", "sent"] + ["d_" + n for n in DMAS]
              + ["arr%d%d" % (s, l) for s in range(2) for l in range(3)])


def transfers_of(T, topo, r):
    n = len(T.cores)
    src = T.cores[r]
    dsts = [(b, T.cores[(r - b) % n]) for b in range(1, NB)]
    out, used = [], set()
    for near in (False, True):
        part = [d for d in dsts if (topo.chip(d[1]) == topo.chip(src)) == near]
        if part:
            es = set.intersection(*[set(topo.engines(src, c)) for _, c in part]) - used
            used |= es
            out.append((sum(1 << e for e in es), len(es), part))
    return out


def arrange(cases, nfirst):
    ops = cases[0][0]
    n = len(ops)
    succ = [[] for _ in range(n)]
    for i, o in enumerate(ops):
        for d in o["deps"]:
            succ[d].append(i)
    eng = ["vspgy".index(o["eng"]) for o in ops]
    tabs = []
    for os_, c in cases:
        gaps = [[(d, c["hop"] if eng[d] != eng[i] or os_[d]["kind"] != "c" else (0.0 if eng[i] == 2 else c["same"]))
                 for d in o["deps"]] for i, o in enumerate(os_)]
        tabs.append(([o["dur"] for o in os_], [o["lat"] for o in os_], gaps))

    def span(seq):
        tot = 0.0
        for dur, lat, gaps in tabs:
            free, fin = [0.0] * 5, [0.0] * n
            for i in seq:
                t = free[eng[i]]
                for d, gp in gaps[i]:
                    x = fin[d] + gp
                    if x > t:
                        t = x
                t += dur[i]
                free[eng[i]] = t
                fin[i] = t + lat[i]
            tot += max(fin)
        return tot / len(tabs)

    dur, lat, gaps = tabs[0]
    togo = [0.0] * n
    for i in range(n - 1, -1, -1):
        togo[i] = dur[i] + lat[i] + max([togo[j] + 0.1 for j in succ[i]] + [0.0])
    left = [len(o["deps"]) for o in ops]
    free, fin, seq = [0.0] * 5, [0.0] * n, []
    cand = {i: 0.0 for i in range(n) if not left[i]}
    while cand:
        i = min(cand, key=lambda j: (j >= nfirst, max(free[eng[j]], cand[j]), -togo[j]))
        free[eng[i]] = max(free[eng[i]], cand.pop(i)) + dur[i]
        fin[i] = free[eng[i]] + lat[i]
        seq.append(i)
        for j in succ[i]:
            left[j] -= 1
            if not left[j]:
                cand[j] = max(fin[d] + gp for d, gp in gaps[j])
    seq = list(range(nfirst)) + seq[nfirst:]
    best = cur = span(seq)
    now, x = seq, 12345
    for it in range(STEPS):
        x = (x * 6364136223846793005 + 1442695040888963407) % 18446744073709551616
        p = nfirst + (x >> 40) % (n - nfirst)
        i = now[p]
        step = 1 if (x >> 30) & 1 else -1
        hops = (1, 1, 1, 2, 3, 5, 1, 2)[(x >> 31) & 7]
        bad = succ[i] if step > 0 else ops[i]["deps"]
        q, to = p + step, None
        while nfirst <= q < n and now[q] not in bad and hops:
            if eng[now[q]] == eng[i]:
                to, hops = q, hops - 1
            q += step
        if to is not None:
            new = now[:p] + now[p + 1:]
            new.insert(to, i)
            val = span(new)
            if val <= cur or ((x >> 8) & 65535) / 65536.0 < math.exp((cur - val) / (0.06 * (1 - it / STEPS) + 1e-4)):
                cur, now = val, new
                if val < best:
                    best, seq = val, new
    return seq, best


def build(g, T, topo, rank, cost):
    V, S, P = g.vector, g.scalar, g.tensor
    ops, writer, readers = [], {}, {}
    cyc, gat = cost["cyc"], cost["gat"]

    def op(eng, dur, fn, reads, writes, kind="c", lat=0.0, sem=None, grp=None):
        deps = {writer[k] for k in reads + writes if k in writer}
        for k in writes:
            deps |= set(readers.get(k, []))
        i = len(ops)
        for k in reads:
            readers.setdefault(k, []).append(i)
        for k in writes:
            writer[k] = i
            readers[k] = []
        ops.append({"eng": eng, "dur": dur, "fn": fn, "deps": sorted(deps), "kind": kind, "lat": lat, "sem": sem, "grp": grp})

    def v(n, fn, reads, writes):
        op("v", cost["vfix"] + n * cyc, lambda last: [fn()], reads, writes)

    def vs(k, n, fn, reads, writes):
        op("v", k * (cost["vfix"] + n * cyc), lambda last: [fn(j) for j in range(k)], reads, writes)

    def s(n, fn, reads, writes):
        op("s", cost["sfix"] + n * cyc, lambda last: [fn()], reads, writes)

    def ss(k, n, fn, reads, writes):
        op("s", k * (cost["sfix"] + n * cyc), lambda last: [fn(j) for j in range(k)], reads, writes)

    def q(t, fn, reads, writes):
        op("g", t, lambda last: [fn()], reads, writes)

    def pe(n, fn, reads, writes, grp=None):
        op("p", n * cost["pe"], fn, reads, writes, grp=grp)

    def dma(eng, name, out, in_, reads, writes, lat):
        qq = g.sync if eng == "y" else S
        op(eng, 0.06, lambda last: qq.dma_start(out, in_), reads, writes, kind="d", lat=lat, sem="d_" + name)

    plan = transfers_of(T, topo, rank)

    def send(src, dst, sem, reads, key, lat):
        op("g", 0.3, lambda last: g.remote_dma_fused([RemoteDMATransfer(
            dst_ids=[DstId(rid=topo.addr(c)[0], pnc=topo.addr(c)[1]) for _, c in part], dma_engine_mask=mask,
            remote_sem=T.sem[sem], srcs=[src], dsts=[dst(b) for b, _ in part]) for mask, _, part in plan],
            local_sem=T.sem.sent), reads, [key], kind="r", lat=lat, sem=sem)

    ts, tt, cp, act, mm = V.tensor_scalar, V.tensor_tensor, V.tensor_copy, S.activation, P.matmul
    dma("y", "lo", T.SM[:, 0:8], T.lo0[:], [], ["lo"], cost["load"])
    dma("s", "hi", T.SM[:, 8:16], T.hi0[:], [], ["hi"], cost["load"])
    dma("y", "home", T.SM[:, 16:48], T.home[:], [], ["home"], cost["load"])
    dma("s", "x", T.X0[:], T.xrow[:], [], ["x"], cost["load"])
    dma("y", "y", T.Y[:], T.ytab[:], [], ["y"], cost["yload"])
    dma("y", "ha", T.HH[:, :, 0, :], T.ha[:], [], ["ha"], cost["yload"])
    dma("y", "hb", T.HH[:, :, 1, :], T.hb[:], [], ["hb"], cost["yload"])

    q(0.2, lambda: g.iota(T.EI[:, 0:32], [[1, 32]], 0, 0, allow_small_or_imprecise_dtypes=True), [], ["ei0"])
    q(0.4, lambda: g.iota(T.T1[:], [[0, 8], [-1, 16]], 128, 1), [], ["t1"])
    q(0.2, lambda: g.iota(T.EI[:, 32:64], [[-1, 32]], 31, 0, allow_small_or_imprecise_dtypes=True), [], ["ei1"])
    v(64, lambda: V.memset(T.ONE[:], 1.0), [], ["one"])
    q(0.45, lambda: g.affine_select(T.BO1[:], T.ONE[:], [[-16, 8], [0, 16]], A.is_ge, 0.0, 0, 1), ["one"], ["bo1"])
    q(0.45, lambda: g.affine_select(T.BO[:], T.BO1[:], [[16, 8], [0, 16]], A.is_ge, 0.0, 15, -1), ["bo1"], ["bo"])
    q(0.45, lambda: g.affine_select(T.ID[:], T.ONE[:], [[-1, 128]], A.is_equal, 0.0, 0, 1), ["one"], ["id"])
    v(32, lambda: ts(T.EPS[:, 0:32], T.EI[:, 0:32], 1.0 / 32, None, A.mult), ["ei0"], ["eps0"])
    v(32, lambda: ts(T.EPS[:, 32:64], T.EI[:, 32:64], 1.0 / 32, None, A.mult), ["ei1"], ["eps1"])
    v(8, lambda: cp(T.C8[:], T.EI[:, 0:8]), ["ei0"], ["c8"])
    v(128, lambda: ts(T.T2[:], T.T1[:], 15, None, A.bitwise_and), ["t1"], ["t2"])
    v(16, lambda: ts(T.DG[:], T.T2[:, 0:16], 0.0, None, A.is_equal), ["t2"], ["dg"])
    v(128, lambda: ts(T.MK[:], T.T2[:], 0.0, None, A.is_equal), ["t2"], ["mk"])
    v(1, lambda: cp(T.PM[:], T.T2[:, 0:1]), ["t2"], ["pm"])
    v(64, lambda: ts(T.NID[:], T.ID[:], -1.0, None, A.mult), ["id"], ["nid"])
    v(8, lambda: cp(T.BI[:], T.BO[:, 0:128:16]), ["bo"], ["bi"])
    v(72, lambda: V.memset(T.W[:], 0.0), [], ["w"])
    v(8, lambda: cp(T.W[:, 15:128:16], T.BO[:, 0:128:16]), ["bo"], ["w"])
    v(256, lambda: V.memset(T.CS[:], 1.0 / 32), [], ["cs"])
    v(8, lambda: V.memset(T.CS[:, 0:256:32], 16384.0), [], ["cs"])

    def xrc(u, c0, c1):
        return T.XR[:, u * RW * 128 + c0:u * RW * 128 + c1]

    def copy(on_s, o, i_, n, ks, kw):
        if on_s:
            s(n, lambda: act(o, i_, F.Copy), ks, kw)
        else:
            v(n / 2, lambda: cp(o, i_), ks, kw)

    def widen(u, h, on_s):
        while h < RW:
            copy(on_s, xrc(u, h * 128, 2 * h * 128), xrc(u, 0, h * 128), h * 128, [("xr", u, j) for j in range(h)],
                 [("xr", u, j) for j in range(h, 2 * h)])
            h *= 2

    def rows_pass1(l):
        for j in range(2):
            copy(l != 0, xrc(l, j * 128, (j + 1) * 128), T.X0[:, l * 128:(l + 1) * 128], 128, ["x"], [("xr", l, j)])
        widen(l, 2, l != 0)

    def sp(u, c0, c1, st=1):
        return T.SP[:, u * 128 + c0:u * 128 + c1:st]

    def offsets_and_home(u, dl, lol, dt_, bt, st, kl, kt):
        def col(c):
            return sp(u, c, c + 1)
        vs(8, 32, lambda j: ts(T.OFF[:, u * 256 + j:(u + 1) * 256:8], T.EPS[:, 0:32], col(dl + st * j), col(lol + st * j),
                               A.mult, A.add), kl + ["eps0"], [("off", u)])
        ss(8, 32, lambda j: act(T.AB[:, u * 256 + j * 32:u * 256 + (j + 1) * 32], T.EPS[:, 32:64], F.Abs,
                                bias=col(bt + j), scale=col(dt_ + st * j)), kt + ["eps1"], [("ab", u)])
        v(256, lambda: ts(T.HF[:, u * 256:(u + 1) * 256], T.AB[:, u * 256:(u + 1) * 256], 1.0 / 16, 1535.53125,
                          A.mult, A.add), [("ab", u)], [("hf", u)])

    v(8, lambda: ts(sp(0, 32, 40), T.SM[:, 0:8], -C0, None, A.add), ["lo"], [("lo", 0)])
    v(16, lambda: tt(sp(0, 64, 72), T.SM[:, 8:16], T.SM[:, 0:8], A.subtract), ["lo", "hi"], [("d", 0)])
    v(8, lambda: ts(sp(0, 72, 80), T.SM[:, 0:8], -C0 - 2048.0, None, A.add), ["lo"], [("loc", 0)])
    v(48, lambda: cp(T.SF[:], T.SM[:]), ["lo", "hi", "home"], ["sf"])
    v(8, lambda: cp(T.BF[:], T.BO[:, 0:128:16]), ["bo"], ["bf"])
    ss(9, 48, lambda k: act(T.Z0[:, k:768:16], T.SF[:], F.Identity, scale=T.DG[:, k:k + 1]), ["sf", "dg"], ["z0"])
    vs(7, 48, lambda k: ts(T.Z0[:, k + 9:768:16], T.SF[:], T.DG[:, k + 9:k + 10], None, A.mult), ["sf", "dg"], ["z1"])
    pe(24 * 64, lambda last: [mm(T.P1[:, j * 8:(j + 1) * 8], T.Z0[:, j * 128:(j + 1) * 128], T.BF[:], True, True)
                              for j in range(6)], ["z0", "z1", "bf"], [("ps", 1)])
    v(16, lambda: ts(T.LT[:], T.P1[:, 0:16], -C0, None, A.add), [("ps", 1)], ["lt"])
    v(32, lambda: cp(T.MT[:], T.P1[:, 16:48]), [("ps", 1)], ["mt"])
    v(16, lambda: tt(sp(0, 88, 96), T.LT[:, 8:16], T.LT[:, 0:8], A.subtract), ["lt"], [("dt", 0)])
    v(16, lambda: tt(sp(0, 80, 88), T.LT[:, 0:8], T.MT[:, 0:8], A.subtract), ["lt", "mt"], [("bt", 0)])
    offsets_and_home(0, 64, 32, 88, 80, 1, [("lo", 0), ("d", 0)], [("dt", 0), ("bt", 0)])
    rows_pass1(0)

    def hints():
        def ht(j):
            return T.HT[:, j * 48:(j + 1) * 48]
        hk = ["ha", "hb", ("sc", 0)]
        v(48, lambda: ts(ht(5), T.HH[:], 15, None, A.bitwise_and), hk, ["h5"])
        v(48, lambda: cp(T.H4[:], ht(5)), ["h5"], ["h4f"])
        v(48, lambda: ts(ht(0), T.HH[:], 2, 0x60, A.logical_shift_right, A.bitwise_and), hk, ["h0"])
        v(48, lambda: ts(ht(1), T.HH[:], 6, 0x18, A.logical_shift_right, A.bitwise_and), hk, ["h1"])
        v(48, lambda: ts(ht(2), T.HH[:], 4, 7, A.logical_shift_right, A.bitwise_and), hk, ["h2"])
        v(96, lambda: tt(ht(3), ht(0), ht(1), A.add), ["h0", "h1"], ["h3"])
        v(96, lambda: tt(ht(4), ht(3), ht(2), A.add), ["h3", "h2"], ["h4"])
        v(48, lambda: cp(T.HOFF[:], ht(4)), ["h4"], ["hoff"])
        ss(16, 48, lambda k: act(T.ZH[:, k:768:16], T.H4[:], F.Identity, scale=T.DG[:, k:k + 1]), ["h4f", "dg"], ["zh"])
        pe(768, lambda last: [mm(T.P0[:, 0:512], T.BO[:], T.ZH[:, 0:512], True, True),
                              mm(T.P0[:, 512:768], T.BO[:], T.ZH[:, 512:768], True, True)], ["zh", "bo"], [("ps", 0)])
        v(768, lambda: ts(T.HM[:], T.P0[:, 0:768], T.PM[:], None, A.is_equal), [("ps", 0), "pm"], ["hm"])
        for l in range(1, 4):
            rows_pass1(l)

    slot = [2]
    held = {}
    PS = [T.P0, T.P1, T.P2]

    def unit(ps, l):
        u = ps * 4 + l
        ub = 0 if l == 0 else u
        K, KEY, G, R = (T.KB, T.PB, T.GB, T.RB) if ps else (T.KA, T.PA, T.GA, T.RA)
        bank = ("key", ps)
        if l > 0:
            zm = T.ZM[:, u * 256:(u + 1) * 256]
            v(256 * gat, lambda: tt(zm, K[:, 0:32 * l].indirect(T.HOFF[:, 16 * (l - 1):16 * l]),
                                    T.HM[:, 256 * (l - 1):256 * l], A.mult),
              ["hoff", "hm"] + [("k", ps, j) for j in range(l)] + [("arr", ps, j) for j in range(l)], [("zm", u)])

            def ends(last):
                r = [mm(KEY[:, 256:288:2], T.W[:, 15 - k:143 - k], T.ZM[:, u * 256 + k:(u + 1) * 256:16], k == 0, k == 15)
                     for k in range(16)]
                r.append(mm(KEY[:, 257:272:2], T.ZM[:, u * 256:u * 256 + 128], T.BI[:], True, True))
                r.append(mm(KEY[:, 273:288:2], T.ZM[:, u * 256 + 128:(u + 1) * 256], T.BI[:], True, True))
                return r
            pe(18 * 64, ends, [("zm", u), "w", "bi"], [bank])
            v(32, lambda: ts(sp(u, 0, 32), KEY[:, 256:288], 2048.0 - C0, None, A.add), [bank], [("uv", u)])
            v(32, lambda: tt(sp(u, 32, 48), sp(u, 0, 16), sp(u, 16, 32), A.min), [("uv", u)], [("lo", u)])
            v(32, lambda: tt(sp(u, 48, 64), sp(u, 0, 16), sp(u, 16, 32), A.max), [("uv", u)], [("hi", u)])
            v(32, lambda: tt(sp(u, 64, 80), sp(u, 48, 64), sp(u, 32, 48), A.subtract), [("lo", u), ("hi", u)], [("d", u)])
            v(16, lambda: tt(sp(u, 80, 88), sp(u, 33, 48, 2), T.MT[:, 8 * l:8 * l + 8], A.subtract), [("lo", u), "mt"], [("bt", u)])
            s(8, lambda: act(sp(u, 88, 96), sp(u, 32, 48, 2), F.Identity, bias=-2048.0), [("lo", u)], [("loc", u)])
            offsets_and_home(u, 64, 32, 65, 80, 2, [("lo", u), ("d", u)], [("d", u), ("bt", u)])
        dlist = sp(0, 64, 72) if l == 0 else sp(u, 64, 80, 2)
        pe(256, lambda last: [mm(KEY[:, 0:256], T.ID[:], T.HF[:, ub * 256:(ub + 1) * 256], True, False)],
           [("hf", ub), "id"], [bank])
        xk = [("xr", u, j) for j in range(RW)]

        def sums(terms, e0, e1, reads):
            def fn(last):
                todo = [(e, t) for e in range(e0, e1) for t in terms]
                return [mm(KEY[:, 31 - e:256:32], t[:, l * 4096 + e * 128:l * 4096 + (e + 1) * 128], T.BI[:],
                           False, last and j == len(todo) - 1) for j, (e, t) in enumerate(todo)]
            pe(64 * len(terms) * (e1 - e0), fn, reads + [bank, "bi"], [], grp=u)

        def items(h, h1):
            return T.Y[:, 0:4096].indirect(T.OFF[:, ub * 256 + h * 8:ub * 256 + h1 * 8])

        def piece(kind, e0, e1):
            n = (e1 - e0) * 128
            c0 = l * 4096 + e0 * 128
            src, r_ = G, R[:, c0:c0 + n]
            gk, rk = [("g", u, e0)], ("r", u, e0)
            if kind == "V2":
                def one(h, h1):
                    v((h1 - h) * 128 * gat, lambda: tt(G[:, l * 4096 + h * 128:l * 4096 + h1 * 128], items(h, h1),
                                                       xrc(u, 0, (h1 - h) * 128), A.subtract),
                      ["y", ("off", ub)] + xk[:h1 - h], [("g", u, h)])
                for h in range(e0, e1, RW):
                    one(h, min(e1, h + RW))
                gk = [("g", u, h) for h in range(e0, e1, RW)]
                held[(u, e0)] = "D"
                v(n / 2, lambda: ts(r_, G[:, c0:c0 + n], 0.0, -2.0, A.min, A.mult), gk, [rk])
                sums([G, R], e0, e1, gk + [rk])
                return
            back = False
            if kind == "S3":
                s(n * gat, lambda: act(G[:, c0:c0 + n], items(e0, e1), F.Copy), ["y", ("off", ub)], gk)
                held[(u, e0)] = "G"
            else:
                src, gk = T.GA, [("g", 0, h) for h in range(e0, e1)]
                back = held[(0, e0)] == "D"
            sl = slot[0] % 3
            slot[0] += 1
            pk = ("ps", sl)

            def diff(last):
                r = []
                for h in range(0, n, 512):
                    m = min(512, n - h)
                    r.append(mm(PS[sl][:, h:h + m], T.ID[:], src[:, c0 + h:c0 + h + m], True, False))
                    if back:
                        r.append(mm(PS[sl][:, h:h + m], T.ID[:], xrc(0, 0, m), False, False))
                    st = 128 if ps else m
                    for c in range(0, m, st):
                        r.append(mm(PS[sl][:, h + c:h + c + st], T.NID[:], xrc(u, 0, st), False, c + st == m))
                return r
            pe(n * (3 if back else 2), diff, gk + ["id", "nid"] + (xk[:1] if ps else xk[:4])
               + ([("xr", 0, j) for j in range(4)] if back else []), [pk])
            s(n, lambda: act(r_, PS[sl][:, 0:n], F.Abs), [pk], [rk])
            sums([R], e0, e1, [rk])

        e = 0
        for kind, ne in PLAN[(ps, l)]:
            piece(kind, e, e + ne)
            e += ne

        fin = T.SC[:, u * 256 + 31:(u + 1) * 256:32]
        ci, ep = T.CI[:, u * 8:u * 8 + 8], T.EP[:, u * 8:u * 8 + 8]
        gm, dw = T.GM[:, u * 128:(u + 1) * 128], T.DW[:, u * 128:(u + 1) * 128]
        own = K[:, 32 * l:32 * l + 8]
        wo = T.WOFF[:, u * 8:u * 8 + 8]
        v(256, lambda: V.tensor_tensor_scan(T.SC[:, u * 256:(u + 1) * 256], T.CS[:], KEY[:, 0:256], 0.0, A.add, A.min),
          ["cs"], [("sc", u), bank])
        v(8, lambda: ts(ci, fin, -C0, None, A.add), [("sc", u)], [("ci", u)])
        v(16, lambda: tt(ep, fin, ci, A.subtract), [("sc", u), ("ci", u)], [("ep", u)])
        v(128 * gat, lambda: tt(gm, ep.indirect(T.C8[:]), T.MK[:], A.mult), [("ep", u), "c8", "mk"], [("gm", u)])
        pe(64, lambda last: [mm(KEY[:, 288:296], gm, T.BI[:], True, True)], [("gm", u), "bi"], [bank])
        v(8, lambda: tt(sp(u, 96, 104), KEY[:, 288:296], dlist, A.mult), [bank, ("d", ub)], [("ed", u)])
        v(16, lambda: tt(own, sp(u, 96, 104), sp(0, 72, 80) if l == 0 else sp(u, 88, 96), A.add),
          [("ed", u), ("loc", ub)], [("k", ps, l)])
        if l < 3:
            send(own, lambda b: K[:, 32 * l + 8 * b:32 * l + 8 * b + 8], "arr%d%d" % (ps, l), [("k", ps, l)],
                 ("arr", ps, l), cost["comm"] if u else cost["comm0"])
        v(8, lambda: ts(wo, own, 2048.0, None, A.add), [("k", ps, l)], [("wo", u)])
        v(128 * gat, lambda: tt(dw, T.Y[:, 0:4096].indirect(wo), xrc(u, 0, 128), A.subtract),
          ["y", ("wo", u), xk[0]], [("dw", u)])
        if ps == 0:
            v(64, lambda: ts(gm, dw, 0.0, -2.0, A.min, A.mult), [("dw", u)], [("gm", u)])
            v(128, lambda: tt(xrc(u + 4, 0, 128), dw, gm, A.add), [("dw", u), ("gm", u)], [("xr", u + 4, 0)])
            v(128, lambda: tt(xrc(u + 4, 128, 256), dw, gm, A.add), [("dw", u), ("gm", u)], [("xr", u + 4, 1)])
            widen(u + 4, 2, False)
        else:
            xo = T.XO[:, l * 128:(l + 1) * 128]
            s(128, lambda: act(xo, dw, F.Abs), [("dw", u)], [("xo", l)])
            dma("s" if l == 3 else "y", "xo%d" % l, T.xo[:, l * 128:(l + 1) * 128], xo, [("xo", l)], [], cost["load"])

    for l in range(4):
        unit(0, l)
        if l == 0:
            hints()
        unit(1, l)
    v(64, lambda: cp(T.AM[:], T.WOFF[:]), [("wo", u) for u in range(8)], ["am"])
    dma("y", "am", T.argm[:], T.AM[:], ["am"], [], cost["load"])
    return ops, list(range(7)), plan


def rank_program(g, core, T, topo):
    rank = T.rank_of(core)
    if rank is None:
        return
    ops, first, plan = build(g, T, topo, rank, COST)
    if not ORDER:
        ORDER["seq"], ORDER["span"] = arrange([(build(g, T, topo, rank, c)[0], c) for c in CASES], len(first))
    seq = ORDER["seq"]
    arrive = sum(k for b in range(1, NB) for _, k, part in transfers_of(T, topo, (rank + b) % len(T.cores))
                 for _, c in part if c == core)
    queue = {"v": g.vector, "s": g.scalar, "p": g.tensor, "g": g, "y": g.sync}
    lastof = {ops[i]["grp"]: i for i in seq}
    count = {"qv": 0, "qs": 0, "qp": 0, "qg": 0}
    seen = {e: {} for e in queue}
    done = {}
    sent = 0
    for i in seq:
        o = ops[i]
        e = o["eng"]
        know = seen[e]
        for d in sorted(o["deps"], key=lambda j: -done[j][1]):
            sem, val, with_it = done[d]
            if (e == "p" and sem == "qp") or know.get(sem, 0) >= val:
                continue
            queue[e].wait_ge(T.sem[sem], val)
            for k2, v2 in with_it.items():
                know[k2] = max(know.get(k2, 0), v2)
            know[sem] = val
        r = o["fn"](lastof[o["grp"]] == i)
        if o["kind"] == "c":
            sem = "q" + e
            for ins in r:
                ins.then_inc(T.sem[sem], 1)
            count[sem] += len(r)
            done[i] = (sem, count[sem], dict(know))
        elif o["kind"] == "d":
            r.then_inc(T.sem[o["sem"]], 16)
            done[i] = (o["sem"], 16, dict(know))
        else:
            sent += sum(k for _, k, _ in plan)
            done[i] = (o["sem"], arrive, {})
    g.wait_ge(T.sem.sent, sent)
    for sem, val in count.items():
        g.sync.wait_ge(T.sem[sem], val)
    for nme in DMAS:
        g.sync.wait_ge(T.sem["d_" + nme], 16)
